import numpy as np, ml_dtypes
CORES = [21,109,149,237,277,365,405,493,150,406]
N = 10
S, B = 2, 256
NT = N * S
def setup_inputs(rng):
    a = (rng.standard_normal((128, 128), dtype=np.float32) / 12).astype(ml_dtypes.bfloat16)
    return {"x": rng.standard_normal((N, 128, S * B), dtype=np.float32).astype(ml_dtypes.bfloat16), "a": np.broadcast_to(a, (N, 128, 128)).copy(), "at": np.broadcast_to(a.T, (N, 128, 128)).copy()}
def setup_inputs_big(rng):
    d = setup_inputs(rng)
    for k in ("x",): d[k] = (d[k].astype(np.float32) * 1048576.0).astype(d[k].dtype)
    return d
def setup_inputs_small(rng):
    d = setup_inputs(rng)
    for k in ("x",): d[k] = (d[k].astype(np.float32) * (1 / 1048576.0)).astype(d[k].dtype)
    return d
def setup_inputs_apart(rng):
    d = setup_inputs(rng)
    f = (10.0 ** rng.permutation(np.linspace(-1.5, 1.5, N))).astype(np.float32).reshape(N, 1, 1)
    for k in ("x",): d[k] = (d[k].astype(np.float32) * f).astype(d[k].dtype)
    return d
def reference(x, a, at):
    A = a[0].astype(np.float64); X = [x[t // S][:, B * (t % S):B * (t % S) + B].astype(np.float64) for t in range(NT)]
    f = [None] * NT; b = [None] * NT; h = np.zeros((128, B))
    for t in range(NT):
        h = A.T @ h + X[t]; f[t] = h
    h = np.zeros((128, B))
    for t in range(NT - 1, -1, -1):
        h = A.T @ h + X[t]; b[t] = h
    return {"y": np.stack([np.concatenate([f[r * S + s] + b[r * S + s] for s in range(S)], axis=1) for r in range(N)]).astype(ml_dtypes.bfloat16)}

@@ -1,0 +1,286 @@
+from concourse.bass import DstId, RemoteDMATransfer
+from concourse.mybir import AluOpType
+
+NB = 256
+NPW = 16
+NLAND = 8
+NOB = 4
+NTMP = 5
+NCS = 72
+NE_RANK = 8
+NE_HUB = 8
+
+SCRATCH = {
+    "xs": ("sbuf", [128, 2 * NB], "bfloat16"),
+    "x2": ("sbuf", [128, 2 * NB], "bfloat16"),
+    "ys": ("sbuf", [128, 2 * NB], "bfloat16"),
+    "pw": ("sbuf", [128, 128 * NPW], "bfloat16"),
+    "pt": ("sbuf", [128, 128 * 4], "bfloat16"),
+    "ob": ("sbuf", [128, NB * NOB], "bfloat16"),
+    "land": ("sbuf", [128, NB * NLAND], "bfloat16"),
+    "pP": ("psum", [128, 512], "float32"),
+    "pY0": ("psum", [128, 512], "float32"),
+    "pY1": ("psum", [128, 512], "float32"),
+}
+for _i in range(NTMP):
+    SCRATCH["pT%d" % _i] = ("psum", [128, 512], "float32")
+SEMAPHORES = ["sent"] + ["r%d" % _i for _i in range(NLAND)] + ["c%d" % _i for _i in range(NCS)]
+
+BLOCKS = {
+    "FA": ("F", 3, (0, 2)), "FB": ("F", 4, (1, 3)), "FC": ("F", 7, (4, 6)), "FD": ("F", 8, (5, 7)),
+    "BA": ("B", 4, (5, 7)), "BB": ("B", 3, (4, 6)), "BC": ("B", 0, (1, 3)), "BE": ("B", 7, (8, 9)),
+}
+for _r in range(10):
+    BLOCKS["L%d" % _r] = ("F", _r + 1, (_r,))
+    BLOCKS["R%d" % _r] = ("B", _r - 1, (_r,))
+ROLES = [
+    (0, [("L0", (1,)), ("FA", (6, 7, 9))]),
+    (0, [("L8", (9,)), ("BE", (0, 1, 2, 3))]),
+    (2, [("R2", (1,)), ("FA", (3, 4, 5, 8))]),
+    (4, [("L4", (5,)), ("FC", (7, 8, 9))]),
+    (4, [("BB", (3, 2))]),
+    (4, [("R9", (8,)), ("BE", (4, 5, 6, 7))]),
+    (6, [("R6", (5,)), ("BB", (1, 0))]),
+    (1, [("L1", (2,)), ("FB", (6, 7, 9))]),
+    (1, [("BC", (0,))]),
+    (3, [("R3", (2,)), ("FB", (4, 5, 8))]),
+    (5, [("L5", (6,)), ("FD", (8, 9))]),
+    (5, [("BA", (4, 3, 2))]),
+    (7, [("R7", (6,)), ("BA", (1, 0))]),
+]
+DIRECT = [("L0", (2,)), ("L1", (3,)), ("L4", (6,)), ("L5", (7,)), ("R2", (0,)), ("R3", (1,)), ("R6", (4,)), ("R7", (5,))]
+
+_CACHE = {}
+
+
+def _parts(name):
+    kind, p, ranks = BLOCKS[name]
+    return [(r, kind, (p - 1 - r) if kind == "F" else (r - p - 1)) for r in ranks]
+
+
+def build_plan(cores, topo):
+    if "plan" in _CACHE:
+        return _CACHE["plan"]
+    cores = list(cores)
+    world = range(4 * topo.CORES_PER_HOST)
+    used = set(cores)
+    hubs = []
+    for anchor, jobs in ROLES:
+        a = cores[anchor]
+        srcs = set(cores[r] for nm, _d in jobs for r, _k, _e in _parts(nm))
+        dsts = set(cores[d] for _nm, ds in jobs for d in ds)
+        cand = [c for c in world if topo.host(c) == topo.host(a) and topo.chip(c) == topo.chip(a) and c not in used
+                and all(topo.may_write(s, c) for s in srcs) and all(topo.may_write(c, d) for d in dsts)]
+        cand.sort(key=lambda c: (topo.die(c) != topo.die(a), -c))
+        used.add(cand[0])
+        hubs.append(cand[0])
+    taken = {}
+
+    def colour(dst_cores):
+        c = 0
+        while any(c in taken.setdefault(d, set()) for d in dst_cores):
+            c += 1
+        for d in dst_cores:
+            taken[d].add(c)
+        return c
+
+    want = {}
+    for h, (_a, jobs) in zip(hubs, ROLES):
+        for nm, _ds in jobs:
+            for r, k, e in _parts(nm):
+                lst = want.setdefault((r, k, e, 0 if e == 0 else 1), [])
+                if h not in lst:
+                    lst.append(h)
+    for nm, ds in DIRECT:
+        r, k, e = _parts(nm)[0]
+        want.setdefault((r, k, e, 2), []).extend(cores[d] for d in ds)
+    sends = dict((r, []) for r in range(len(cores)))
+    at_hub = {}
+    eat = dict((r, []) for r in range(len(cores)))
+    for key in sorted(want, key=lambda q: (q[3], q[2], q[1], q[0])):
+        r, k, e, cls = key
+        col = colour(want[key])
+        sends[r].append((k, e, want[key], col))
+        for d in want[key]:
+            if cls == 2:
+                dr = cores.index(d)
+                eat[dr].append((1, col, NE_RANK, k, abs(dr - r) - 1))
+            else:
+                at_hub[(d, r, k, e)] = col
+    jobs_of = {}
+    for h, (_a, jobs) in zip(hubs, ROLES):
+        out = []
+        for j, (nm, ds) in enumerate(jobs):
+            kind, p, _rk = BLOCKS[nm]
+            dc = [cores[d] for d in ds]
+            col = colour(dc)
+            out.append(([at_hub[(h, r, k, e)] for r, k, e in _parts(nm)], dc, col))
+            emax = max(e for _r, _k, e in _parts(nm))
+            for i, d in enumerate(ds):
+                eat[d].append((2 + emax + 0.5 * j + 0.1 * i, col, NE_HUB, kind, abs(d - p)))
+        jobs_of[h] = out
+    for r in eat:
+        eat[r].sort()
+    plan = {"sends": sends, "jobs": jobs_of, "eat": eat}
+    _CACHE["plan"] = plan
+    return plan
+
+
+def _write(g, core, T, topo, srcs, dst_cores, slot, n_eng):
+    m = topo.mask(core, dst_cores[0])
+    for d in dst_cores:
+        m &= topo.mask(core, d)
+    mask, n, b = 0, 0, 1
+    while n < n_eng:
+        if m & b:
+            mask |= b
+            n += 1
+        b <<= 1
+    ids = []
+    for d in dst_cores:
+        rid, pid = topo.addr(d, core)
+        ids.append(DstId(rid=rid, pnc=pid))
+    tr = RemoteDMATransfer(dst_ids=ids, dma_engine_mask=mask, remote_sem=T.sem["r%d" % slot], srcs=srcs,
+                           dsts=[T.land[:, slot * NB:(slot + 1) * NB] for _d in dst_cores], alu_op=1 if len(srcs) > 1 else 0)
+    g.remote_dma_fused([tr], local_sem=T.sem.sent)
+    return n_eng
+
+
+def rank_program(g, core, T, topo):
+    plan = build_plan(T.cores, topo)
+    if core in plan["jobs"]:
+        total, seen = 0, set()
+        for slots, dst_cores, col in plan["jobs"][core]:
+            for s in slots:
+                if s not in seen:
+                    g.wait_ge(T.sem["r%d" % s], NE_RANK)
+                    seen.add(s)
+            total += _write(g, core, T, topo, [T.land[:, s * NB:(s + 1) * NB] for s in slots], dst_cores, col, NE_HUB)
+        g.wait_ge(T.sem.sent, total)
+        return
+    rank = T.rank_of(core)
+    if rank is None:
+        return
+    te, ve, sy, sc = g.tensor, g.vector, g.sync, g.scalar
+    sends, eat = plan["sends"][rank], plan["eat"][rank]
+    cnt = [0]
+    done = {}
+    made = []
+
+    def new(val=1):
+        cnt[0] += 1
+        made.append(("c%d" % (cnt[0] - 1), val))
+        return made[-1]
+
+    def wait(q, s):
+        if (q, s[0]) not in done:
+            done[(q, s[0])] = 1
+            {"te": te, "ve": ve, "sy": sy, "sc": sc, "g": g}[q].wait_ge(T.sem[s[0]], s[1])
+
+    def inc(ins, s):
+        ins.then_inc(T.sem[s[0]], s[1])
+        return s
+
+    def A(n, m=None):
+        return T.pw[:, (n - 1) * 128:(m or n) * 128]
+
+    x0, x1 = T.xs[:, 0:NB], T.xs[:, NB:2 * NB]
+    sx = inc(sy.dma_start(T.xs[:], T.x[:]), new(16))
+    okA = {1: inc(sc.dma_start(A(1), T.a[:]), new(16))}
+    okT = {1: inc(sc.dma_start(T.pt[:, 0:128], T.at[:]), new(16))}
+    ptcol = {1: 0, 2: 1, 4: 2, 8: 3}
+
+    wait("te", sx)
+    wait("te", okA[1])
+    sP = inc(te.matmul(T.pP[:, 0:2 * NB], A(1), T.xs[:], True, True), new())
+    obcol, okB = {}, {}
+
+    def ob(key):
+        if key not in obcol:
+            obcol[key] = len(obcol)
+        return T.ob[:, obcol[key] * NB:(obcol[key] + 1) * NB]
+
+    wait("ve", sP)
+    wait("ve", sx)
+    for k, _e, _d, _c in sends:
+        if (k, 0) not in okB:
+            pp, xx = (T.pP[:, 0:NB], x1) if k == "F" else (T.pP[:, NB:2 * NB], x0)
+            okB[(k, 0)] = inc(ve.tensor_tensor(ob((k, 0)), pp, xx, AluOpType.add), new())
+
+    banks = [["pT%d" % i, []] for i in range(NTMP)]
+    turn = [0]
+
+    def product(lhsT, rhs, cols, needs, out):
+        bank = banks[turn[0] % NTMP]
+        turn[0] += 1
+        for s in needs + bank[1]:
+            wait("te", s)
+        sm = inc(te.matmul(T[bank[0]][:, 0:cols], lhsT, rhs, True, True), new())
+        wait("ve", sm)
+        so = inc(ve.tensor_copy(out, T[bank[0]][:, 0:cols]), new())
+        bank[1] = [so]
+        return so
+
+    top = max([2 * k + 2 for _s, _c, _n, _kd, k in eat] + [2 * e for _k, e, _d, _c in sends])
+    todo = sorted(set((e, k) for k, e, _d, _c in sends if e > 0))
+
+    def premultiply(have):
+        for e, k in list(todo):
+            if 2 * e <= have:
+                todo.remove((e, k))
+                okB[(k, e)] = product(A(2 * e), ob((k, 0)), NB, [okA[2 * e], okB[(k, 0)]], ob((k, e)))
+
+    m, have = 1, 1
+    while have < top:
+        hi = min(2 * m, top)
+        tm = T.pt[:, ptcol[m] * 128:(ptcol[m] + 1) * 128]
+        lo = m + 1
+        while lo <= hi:
+            up = min(lo + 3, hi)
+            s = product(tm, A(lo - m, up - m), 128 * (up - lo + 1), [okT[m]] + [okA[i - m] for i in range(lo, up + 1)], A(lo, up))
+            for i in range(lo, up + 1):
+                okA[i] = s
+            lo = up + 1
+        have = hi
+        premultiply(have)
+        if 2 * m < top:
+            okT[2 * m] = product(A(m), tm, 128, [okA[m], okT[m]], T.pt[:, ptcol[2 * m] * 128:(ptcol[2 * m] + 1) * 128])
+        m *= 2
+
+    total = 0
+    for k, e, dst_cores, col in sends:
+        wait("g", okB[(k, e)])
+        total += _write(g, core, T, topo, [ob((k, e))], dst_cores, col, NE_RANK)
+
+    s2 = inc(ve.tensor_tensor(T.x2[:], T.xs[:], T.xs[:], AluOpType.add), new())
+
+    Y0, Y1 = T.pY0[:, 0:NB], T.pY1[:, 0:NB]
+    te.matmul(Y0, A(1), x1, True, False)
+    te.matmul(Y1, A(1), x0, True, False)
+    sY0 = sY1 = None
+    for i, (_sc, col, n_eng, kind, k) in enumerate(eat):
+        last = i == len(eat) - 1
+        wait("te", okA[2 * k + 1])
+        wait("te", okA[2 * k + 2])
+        te.wait_ge(T.sem["r%d" % col], n_eng)
+        blk = T.land[:, col * NB:(col + 1) * NB]
+        e0, e1 = (2 * k + 1, 2 * k + 2) if kind == "F" else (2 * k + 2, 2 * k + 1)
+        i0 = te.matmul(Y0, A(e0), blk, False, last)
+        if last:
+            sY0 = inc(i0, new())
+        i1 = te.matmul(Y1, A(e1), blk, False, last)
+        if last:
+            sY1 = inc(i1, new())
+    wait("ve", s2)
+    wait("ve", sY0)
+    f0 = inc(ve.tensor_tensor(T.ys[:, 0:NB], Y0, T.x2[:, 0:NB], AluOpType.add), new())
+    wait("ve", sY1)
+    f1 = inc(ve.tensor_tensor(T.ys[:, NB:2 * NB], Y1, T.x2[:, NB:2 * NB], AluOpType.add), new())
+    wait("sy", f0)
+    wait("sy", inc(sy.dma_start(T.y[:, 0:NB], T.ys[:, 0:NB]), new(16)))
+    wait("sc", f1)
+    wait("sc", inc(sc.dma_start(T.y[:, NB:2 * NB], T.ys[:, NB:2 * NB]), new(16)))
+    g.wait_ge(T.sem.sent, total)
+    for s in made:
+        if not any(name == s[0] for _q, name in done):
+            wait("g", s)

@@ -5,10 +5,9 @@ NB = 256
 NPW = 16
 NLAND = 8
 NOB = 4
-NTMP = 5
+NTMP = 4
 NCS = 72
-NE_RANK = 8
-NE_HUB = 8
+NPOOL = 8
 
 SCRATCH = {
     "xs": ("sbuf", [128, 2 * NB], "bfloat16"),
@@ -19,6 +18,7 @@ SCRATCH = {
     "ob": ("sbuf", [128, NB * NOB], "bfloat16"),
     "land": ("sbuf", [128, NB * NLAND], "bfloat16"),
     "pP": ("psum", [128, 512], "float32"),
+    "pQ": ("psum", [128, 512], "float32"),
     "pY0": ("psum", [128, 512], "float32"),
     "pY1": ("psum", [128, 512], "float32"),
 }
@@ -34,19 +34,19 @@ for _r in range(10):
     BLOCKS["L%d" % _r] = ("F", _r + 1, (_r,))
     BLOCKS["R%d" % _r] = ("B", _r - 1, (_r,))
 ROLES = [
-    (0, [("L0", (1,)), ("FA", (6, 7, 9))]),
-    (0, [("L8", (9,)), ("BE", (0, 1, 2, 3))]),
-    (2, [("R2", (1,)), ("FA", (3, 4, 5, 8))]),
-    (4, [("L4", (5,)), ("FC", (7, 8, 9))]),
-    (4, [("BB", (3, 2))]),
-    (4, [("R9", (8,)), ("BE", (4, 5, 6, 7))]),
-    (6, [("R6", (5,)), ("BB", (1, 0))]),
-    (1, [("L1", (2,)), ("FB", (6, 7, 9))]),
-    (1, [("BC", (0,))]),
-    (3, [("R3", (2,)), ("FB", (4, 5, 8))]),
-    (5, [("L5", (6,)), ("FD", (8, 9))]),
-    (5, [("BA", (4, 3, 2))]),
-    (7, [("R7", (6,)), ("BA", (1, 0))]),
+    (0, [("L0", (1,)), ("FA", (6, 7, 9))], 1),
+    (0, [("L8", (9,)), ("BE", (0, 1, 2, 3))], 0),
+    (2, [("R2", (1,)), ("FA", (3, 4, 5, 8))], 0),
+    (4, [("L4", (5,)), ("FC", (7, 8, 9))], 0),
+    (4, [("BB", (3, 2))], 0),
+    (4, [("R9", (8,)), ("BE", (4, 5, 6, 7))], 1),
+    (6, [("R6", (5,)), ("BB", (1, 0))], 1),
+    (1, [("L1", (2,)), ("FB", (6, 7, 9))], 0),
+    (1, [("BC", (0,))], 1),
+    (3, [("R3", (2,)), ("FB", (4, 5, 8))], 1),
+    (5, [("L5", (6,)), ("FD", (8, 9))], 1),
+    (5, [("BA", (4, 3, 2))], 1),
+    (7, [("R7", (6,)), ("BA", (1, 0))], 1),
 ]
 DIRECT = [("L0", (2,)), ("L1", (3,)), ("L4", (6,)), ("L5", (7,)), ("R2", (0,)), ("R3", (1,)), ("R6", (4,)), ("R7", (5,))]
 
@@ -58,6 +58,10 @@ def _parts(name):
     return [(r, kind, (p - 1 - r) if kind == "F" else (r - p - 1)) for r in ranks]
 
 
+def _same_chip(topo, a, b):
+    return (topo.host(a), topo.chip(a)) == (topo.host(b), topo.chip(b))
+
+
 def build_plan(cores, topo):
     if "plan" in _CACHE:
         return _CACHE["plan"]
@@ -65,13 +69,13 @@ def build_plan(cores, topo):
     world = range(4 * topo.CORES_PER_HOST)
     used = set(cores)
     hubs = []
-    for anchor, jobs in ROLES:
+    for anchor, jobs, other in ROLES:
         a = cores[anchor]
         srcs = set(cores[r] for nm, _d in jobs for r, _k, _e in _parts(nm))
         dsts = set(cores[d] for _nm, ds in jobs for d in ds)
-        cand = [c for c in world if topo.host(c) == topo.host(a) and topo.chip(c) == topo.chip(a) and c not in used
+        cand = [c for c in world if _same_chip(topo, c, a) and c not in used
                 and all(topo.may_write(s, c) for s in srcs) and all(topo.may_write(c, d) for d in dsts)]
-        cand.sort(key=lambda c: (topo.die(c) != topo.die(a), -c))
+        cand.sort(key=lambda c: ((topo.die(c) != topo.die(a)) != bool(other), -c))
         used.add(cand[0])
         hubs.append(cand[0])
     taken = {}
@@ -85,7 +89,7 @@ def build_plan(cores, topo):
         return c
 
     want = {}
-    for h, (_a, jobs) in zip(hubs, ROLES):
+    for h, (_a, jobs, _o) in zip(hubs, ROLES):
         for nm, _ds in jobs:
             for r, k, e in _parts(nm):
                 lst = want.setdefault((r, k, e, 0 if e == 0 else 1), [])
@@ -99,16 +103,17 @@ def build_plan(cores, topo):
     eat = dict((r, []) for r in range(len(cores)))
     for key in sorted(want, key=lambda q: (q[3], q[2], q[1], q[0])):
         r, k, e, cls = key
+        want[key].sort(key=lambda d: _same_chip(topo, d, cores[r]))
         col = colour(want[key])
         sends[r].append((k, e, want[key], col))
         for d in want[key]:
             if cls == 2:
                 dr = cores.index(d)
-                eat[dr].append((1, col, NE_RANK, k, abs(dr - r) - 1))
+                eat[dr].append((1, col, k, abs(dr - r) - 1))
             else:
                 at_hub[(d, r, k, e)] = col
     jobs_of = {}
-    for h, (_a, jobs) in zip(hubs, ROLES):
+    for h, (_a, jobs, _o) in zip(hubs, ROLES):
         out = []
         for j, (nm, ds) in enumerate(jobs):
             kind, p, _rk = BLOCKS[nm]
@@ -117,45 +122,58 @@ def build_plan(cores, topo):
             out.append(([at_hub[(h, r, k, e)] for r, k, e in _parts(nm)], dc, col))
             emax = max(e for _r, _k, e in _parts(nm))
             for i, d in enumerate(ds):
-                eat[d].append((2 + emax + 0.5 * j + 0.1 * i, col, NE_HUB, kind, abs(d - p)))
+                eat[d].append((2 + emax + 0.5 * j + 0.1 * i, col, kind, abs(d - p)))
         jobs_of[h] = out
     for r in eat:
         eat[r].sort()
-    plan = {"sends": sends, "jobs": jobs_of, "eat": eat}
+    n_of = {}
+    inc = {}
+    calls = [(cores[r], [(ds, col) for _k, _e, ds, col in sends[r]]) for r in sends]
+    calls += [(h, [(ds, col) for _s, ds, col in jobs_of[h]]) for h in jobs_of]
+    for c, lst in calls:
+        for on in (False, True):
+            cnt = sum(1 for ds, _col in lst for d in ds if _same_chip(topo, c, d) == on and (c in jobs_of or d in jobs_of))
+            n_of[(c, on)] = NPOOL // 2 if cnt <= 2 else NPOOL // 4
+        for ds, col in lst:
+            for d in ds:
+                inc[(d, col)] = n_of[(c, _same_chip(topo, c, d))]
+    plan = {"sends": sends, "jobs": jobs_of, "eat": eat, "n_of": n_of, "inc": inc}
     _CACHE["plan"] = plan
     return plan
 
 
-def _write(g, core, T, topo, srcs, dst_cores, slot, n_eng):
-    m = topo.mask(core, dst_cores[0])
+def _write(g, core, T, topo, plan, turn, srcs, dst_cores, slot):
+    total = 0
     for d in dst_cores:
-        m &= topo.mask(core, d)
-    mask, n, b = 0, 0, 1
-    while n < n_eng:
-        if m & b:
-            mask |= b
-            n += 1
-        b <<= 1
-    ids = []
-    for d in dst_cores:
+        on = _same_chip(topo, core, d)
+        n = plan["n_of"][(core, on)]
+        m = topo.mask(core, d)
+        bits = [b for b in range(m.bit_length()) if (m >> b) & 1]
+        pool = bits[-NPOOL:] if on else bits[:NPOOL]
+        gi = turn[on] % (NPOOL // n)
+        turn[on] += 1
+        mask = 0
+        for b in pool[gi * n:(gi + 1) * n]:
+            mask |= 1 << b
         rid, pid = topo.addr(d, core)
-        ids.append(DstId(rid=rid, pnc=pid))
-    tr = RemoteDMATransfer(dst_ids=ids, dma_engine_mask=mask, remote_sem=T.sem["r%d" % slot], srcs=srcs,
-                           dsts=[T.land[:, slot * NB:(slot + 1) * NB] for _d in dst_cores], alu_op=1 if len(srcs) > 1 else 0)
-    g.remote_dma_fused([tr], local_sem=T.sem.sent)
-    return n_eng
+        tr = RemoteDMATransfer(dst_ids=[DstId(rid=rid, pnc=pid)], dma_engine_mask=mask, remote_sem=T.sem["r%d" % slot],
+                               srcs=srcs, dsts=[T.land[:, slot * NB:(slot + 1) * NB]], alu_op=1 if len(srcs) > 1 else 0)
+        g.remote_dma_fused([tr], local_sem=T.sem.sent)
+        total += n
+    return total
 
 
 def rank_program(g, core, T, topo):
     plan = build_plan(T.cores, topo)
+    groups = {False: 0, True: 0}
     if core in plan["jobs"]:
         total, seen = 0, set()
         for slots, dst_cores, col in plan["jobs"][core]:
             for s in slots:
                 if s not in seen:
-                    g.wait_ge(T.sem["r%d" % s], NE_RANK)
+                    g.wait_ge(T.sem["r%d" % s], plan["inc"][(core, s)])
                     seen.add(s)
-            total += _write(g, core, T, topo, [T.land[:, s * NB:(s + 1) * NB] for s in slots], dst_cores, col, NE_HUB)
+            total += _write(g, core, T, topo, plan, groups, [T.land[:, s * NB:(s + 1) * NB] for s in slots], dst_cores, col)
         g.wait_ge(T.sem.sent, total)
         return
     rank = T.rank_of(core)
@@ -192,7 +210,6 @@ def rank_program(g, core, T, topo):
 
     wait("te", sx)
     wait("te", okA[1])
-    sP = inc(te.matmul(T.pP[:, 0:2 * NB], A(1), T.xs[:], True, True), new())
     obcol, okB = {}, {}
 
     def ob(key):
@@ -200,12 +217,13 @@ def rank_program(g, core, T, topo):
             obcol[key] = len(obcol)
         return T.ob[:, obcol[key] * NB:(obcol[key] + 1) * NB]
 
-    wait("ve", sP)
-    wait("ve", sx)
     for k, _e, _d, _c in sends:
         if (k, 0) not in okB:
-            pp, xx = (T.pP[:, 0:NB], x1) if k == "F" else (T.pP[:, NB:2 * NB], x0)
-            okB[(k, 0)] = inc(ve.tensor_tensor(ob((k, 0)), pp, xx, AluOpType.add), new())
+            bank = (T.pQ if okB else T.pP)[:, 0:NB]
+            xin, xadd = (x0, x1) if k == "F" else (x1, x0)
+            wait("ve", inc(te.matmul(bank, A(1), xin, True, True), new()))
+            wait("ve", sx)
+            okB[(k, 0)] = inc(ve.tensor_tensor(ob((k, 0)), bank, xadd, AluOpType.add), new())
 
     banks = [["pT%d" % i, []] for i in range(NTMP)]
     turn = [0]
@@ -221,7 +239,7 @@ def rank_program(g, core, T, topo):
         bank[1] = [so]
         return so
 
-    top = max([2 * k + 2 for _s, _c, _n, _kd, k in eat] + [2 * e for _k, e, _d, _c in sends])
+    top = max([2 * k + 2 for _s, _c, _kd, k in eat] + [2 * e for _k, e, _d, _c in sends])
     todo = sorted(set((e, k) for k, e, _d, _c in sends if e > 0))
 
     def premultiply(have):
@@ -250,7 +268,7 @@ def rank_program(g, core, T, topo):
     total = 0
     for k, e, dst_cores, col in sends:
         wait("g", okB[(k, e)])
-        total += _write(g, core, T, topo, [ob((k, e))], dst_cores, col, NE_RANK)
+        total += _write(g, core, T, topo, plan, groups, [ob((k, e))], dst_cores, col)
 
     s2 = inc(ve.tensor_tensor(T.x2[:], T.xs[:], T.xs[:], AluOpType.add), new())
 
@@ -258,11 +276,11 @@ def rank_program(g, core, T, topo):
     te.matmul(Y0, A(1), x1, True, False)
     te.matmul(Y1, A(1), x0, True, False)
     sY0 = sY1 = None
-    for i, (_sc, col, n_eng, kind, k) in enumerate(eat):
+    for i, (_sc, col, kind, k) in enumerate(eat):
         last = i == len(eat) - 1
         wait("te", okA[2 * k + 1])
         wait("te", okA[2 * k + 2])
-        te.wait_ge(T.sem["r%d" % col], n_eng)
+        te.wait_ge(T.sem["r%d" % col], plan["inc"][(core, col)])
         blk = T.land[:, col * NB:(col + 1) * NB]
         e0, e1 = (2 * k + 1, 2 * k + 2) if kind == "F" else (2 * k + 2, 2 * k + 1)
         i0 = te.matmul(Y0, A(e0), blk, False, last)

from concourse.bass import DstId, RemoteDMATransfer
from concourse.mybir import AluOpType

NB = 256
NPW = 16
NLAND = 8
NOB = 4
NTMP = 4
NCS = 72
NPOOL = 8

SCRATCH = {
    "xs": ("sbuf", [128, 2 * NB], "bfloat16"),
    "x2": ("sbuf", [128, 2 * NB], "bfloat16"),
    "ys": ("sbuf", [128, 2 * NB], "bfloat16"),
    "pw": ("sbuf", [128, 128 * NPW], "bfloat16"),
    "pt": ("sbuf", [128, 128 * 4], "bfloat16"),
    "ob": ("sbuf", [128, NB * NOB], "bfloat16"),
    "land": ("sbuf", [128, NB * NLAND], "bfloat16"),
    "pP": ("psum", [128, 512], "float32"),
    "pQ": ("psum", [128, 512], "float32"),
    "pY0": ("psum", [128, 512], "float32"),
    "pY1": ("psum", [128, 512], "float32"),
}
for _i in range(NTMP):
    SCRATCH["pT%d" % _i] = ("psum", [128, 512], "float32")
SEMAPHORES = ["sent"] + ["r%d" % _i for _i in range(NLAND)] + ["c%d" % _i for _i in range(NCS)]

BLOCKS = {
    "FA": ("F", 3, (0, 2)), "FB": ("F", 4, (1, 3)), "FC": ("F", 7, (4, 6)), "FD": ("F", 8, (5, 7)),
    "BA": ("B", 4, (5, 7)), "BB": ("B", 3, (4, 6)), "BC": ("B", 0, (1, 3)), "BE": ("B", 7, (8, 9)),
}
for _r in range(10):
    BLOCKS["L%d" % _r] = ("F", _r + 1, (_r,))
    BLOCKS["R%d" % _r] = ("B", _r - 1, (_r,))
ROLES = [
    (0, [("L0", (1,)), ("FA", (6, 7, 9))], 1),
    (0, [("L8", (9,)), ("BE", (0, 1, 2, 3))], 0),
    (2, [("R2", (1,)), ("FA", (3, 4, 5, 8))], 0),
    (4, [("L4", (5,)), ("FC", (7, 8, 9))], 0),
    (4, [("BB", (3, 2))], 0),
    (4, [("R9", (8,)), ("BE", (4, 5, 6, 7))], 1),
    (6, [("R6", (5,)), ("BB", (1, 0))], 1),
    (1, [("L1", (2,)), ("FB", (6, 7, 9))], 0),
    (1, [("BC", (0,))], 1),
    (3, [("R3", (2,)), ("FB", (4, 5, 8))], 1),
    (5, [("L5", (6,)), ("FD", (8, 9))], 1),
    (5, [("BA", (4, 3, 2))], 1),
    (7, [("R7", (6,)), ("BA", (1, 0))], 1),
]
DIRECT = [("L0", (2,)), ("L1", (3,)), ("L4", (6,)), ("L5", (7,)), ("R2", (0,)), ("R3", (1,)), ("R6", (4,)), ("R7", (5,))]

_CACHE = {}


def _parts(name):
    kind, p, ranks = BLOCKS[name]
    return [(r, kind, (p - 1 - r) if kind == "F" else (r - p - 1)) for r in ranks]


def _same_chip(topo, a, b):
    return (topo.host(a), topo.chip(a)) == (topo.host(b), topo.chip(b))


def build_plan(cores, topo):
    if "plan" in _CACHE:
        return _CACHE["plan"]
    cores = list(cores)
    world = range(4 * topo.CORES_PER_HOST)
    used = set(cores)
    hubs = []
    for anchor, jobs, other in ROLES:
        a = cores[anchor]
        srcs = set(cores[r] for nm, _d in jobs for r, _k, _e in _parts(nm))
        dsts = set(cores[d] for _nm, ds in jobs for d in ds)
        cand = [c for c in world if _same_chip(topo, c, a) and c not in used
                and all(topo.may_write(s, c) for s in srcs) and all(topo.may_write(c, d) for d in dsts)]
        cand.sort(key=lambda c: ((topo.die(c) != topo.die(a)) != bool(other), -c))
        used.add(cand[0])
        hubs.append(cand[0])
    taken = {}

    def colour(dst_cores):
        c = 0
        while any(c in taken.setdefault(d, set()) for d in dst_cores):
            c += 1
        for d in dst_cores:
            taken[d].add(c)
        return c

    want = {}
    for h, (_a, jobs, _o) in zip(hubs, ROLES):
        for nm, _ds in jobs:
            for r, k, e in _parts(nm):
                lst = want.setdefault((r, k, e, 0 if e == 0 else 1), [])
                if h not in lst:
                    lst.append(h)
    for nm, ds in DIRECT:
        r, k, e = _parts(nm)[0]
        want.setdefault((r, k, e, 2), []).extend(cores[d] for d in ds)
    sends = dict((r, []) for r in range(len(cores)))
    at_hub = {}
    eat = dict((r, []) for r in range(len(cores)))
    for key in sorted(want, key=lambda q: (q[3], q[2], q[1], q[0])):
        r, k, e, cls = key
        want[key].sort(key=lambda d: _same_chip(topo, d, cores[r]))
        col = colour(want[key])
        sends[r].append((k, e, want[key], col))
        for d in want[key]:
            if cls == 2:
                dr = cores.index(d)
                eat[dr].append((1, col, k, abs(dr - r) - 1))
            else:
                at_hub[(d, r, k, e)] = col
    jobs_of = {}
    for h, (_a, jobs, _o) in zip(hubs, ROLES):
        out = []
        for j, (nm, ds) in enumerate(jobs):
            kind, p, _rk = BLOCKS[nm]
            dc = [cores[d] for d in ds]
            col = colour(dc)
            out.append(([at_hub[(h, r, k, e)] for r, k, e in _parts(nm)], dc, col))
            emax = max(e for _r, _k, e in _parts(nm))
            for i, d in enumerate(ds):
                eat[d].append((2 + emax + 0.5 * j + 0.1 * i, col, kind, abs(d - p)))
        jobs_of[h] = out
    for r in eat:
        eat[r].sort()
    n_of = {}
    inc = {}
    calls = [(cores[r], [(ds, col) for _k, _e, ds, col in sends[r]]) for r in sends]
    calls += [(h, [(ds, col) for _s, ds, col in jobs_of[h]]) for h in jobs_of]
    for c, lst in calls:
        for on in (False, True):
            cnt = sum(1 for ds, _col in lst for d in ds if _same_chip(topo, c, d) == on and (c in jobs_of or d in jobs_of))
            n_of[(c, on)] = NPOOL // 2 if cnt <= 2 else NPOOL // 4
        for ds, col in lst:
            for d in ds:
                inc[(d, col)] = n_of[(c, _same_chip(topo, c, d))]
    plan = {"sends": sends, "jobs": jobs_of, "eat": eat, "n_of": n_of, "inc": inc}
    _CACHE["plan"] = plan
    return plan


def _write(g, core, T, topo, plan, turn, srcs, dst_cores, slot):
    total = 0
    for d in dst_cores:
        on = _same_chip(topo, core, d)
        n = plan["n_of"][(core, on)]
        m = topo.mask(core, d)
        bits = [b for b in range(m.bit_length()) if (m >> b) & 1]
        pool = bits[-NPOOL:] if on else bits[:NPOOL]
        gi = turn[on] % (NPOOL // n)
        turn[on] += 1
        mask = 0
        for b in pool[gi * n:(gi + 1) * n]:
            mask |= 1 << b
        rid, pid = topo.addr(d, core)
        tr = RemoteDMATransfer(dst_ids=[DstId(rid=rid, pnc=pid)], dma_engine_mask=mask, remote_sem=T.sem["r%d" % slot],
                               srcs=srcs, dsts=[T.land[:, slot * NB:(slot + 1) * NB]], alu_op=1 if len(srcs) > 1 else 0)
        g.remote_dma_fused([tr], local_sem=T.sem.sent)
        total += n
    return total


def rank_program(g, core, T, topo):
    plan = build_plan(T.cores, topo)
    groups = {False: 0, True: 0}
    if core in plan["jobs"]:
        total, seen = 0, set()
        for slots, dst_cores, col in plan["jobs"][core]:
            for s in slots:
                if s not in seen:
                    g.wait_ge(T.sem["r%d" % s], plan["inc"][(core, s)])
                    seen.add(s)
            total += _write(g, core, T, topo, plan, groups, [T.land[:, s * NB:(s + 1) * NB] for s in slots], dst_cores, col)
        g.wait_ge(T.sem.sent, total)
        return
    rank = T.rank_of(core)
    if rank is None:
        return
    te, ve, sy, sc = g.tensor, g.vector, g.sync, g.scalar
    sends, eat = plan["sends"][rank], plan["eat"][rank]
    cnt = [0]
    done = {}
    made = []

    def new(val=1):
        cnt[0] += 1
        made.append(("c%d" % (cnt[0] - 1), val))
        return made[-1]

    def wait(q, s):
        if (q, s[0]) not in done:
            done[(q, s[0])] = 1
            {"te": te, "ve": ve, "sy": sy, "sc": sc, "g": g}[q].wait_ge(T.sem[s[0]], s[1])

    def inc(ins, s):
        ins.then_inc(T.sem[s[0]], s[1])
        return s

    def A(n, m=None):
        return T.pw[:, (n - 1) * 128:(m or n) * 128]

    x0, x1 = T.xs[:, 0:NB], T.xs[:, NB:2 * NB]
    sx = inc(sy.dma_start(T.xs[:], T.x[:]), new(16))
    okA = {1: inc(sc.dma_start(A(1), T.a[:]), new(16))}
    okT = {1: inc(sc.dma_start(T.pt[:, 0:128], T.at[:]), new(16))}
    ptcol = {1: 0, 2: 1, 4: 2, 8: 3}

    wait("te", sx)
    wait("te", okA[1])
    obcol, okB = {}, {}

    def ob(key):
        if key not in obcol:
            obcol[key] = len(obcol)
        return T.ob[:, obcol[key] * NB:(obcol[key] + 1) * NB]

    for k, _e, _d, _c in sends:
        if (k, 0) not in okB:
            bank = (T.pQ if okB else T.pP)[:, 0:NB]
            xin, xadd = (x0, x1) if k == "F" else (x1, x0)
            wait("ve", inc(te.matmul(bank, A(1), xin, True, True), new()))
            wait("ve", sx)
            okB[(k, 0)] = inc(ve.tensor_tensor(ob((k, 0)), bank, xadd, AluOpType.add), new())

    banks = [["pT%d" % i, []] for i in range(NTMP)]
    turn = [0]

    def product(lhsT, rhs, cols, needs, out):
        bank = banks[turn[0] % NTMP]
        turn[0] += 1
        for s in needs + bank[1]:
            wait("te", s)
        sm = inc(te.matmul(T[bank[0]][:, 0:cols], lhsT, rhs, True, True), new())
        wait("ve", sm)
        so = inc(ve.tensor_copy(out, T[bank[0]][:, 0:cols]), new())
        bank[1] = [so]
        return so

    top = max([2 * k + 2 for _s, _c, _kd, k in eat] + [2 * e for _k, e, _d, _c in sends])
    todo = sorted(set((e, k) for k, e, _d, _c in sends if e > 0))

    def premultiply(have):
        for e, k in list(todo):
            if 2 * e <= have:
                todo.remove((e, k))
                okB[(k, e)] = product(A(2 * e), ob((k, 0)), NB, [okA[2 * e], okB[(k, 0)]], ob((k, e)))

    m, have = 1, 1
    while have < top:
        hi = min(2 * m, top)
        tm = T.pt[:, ptcol[m] * 128:(ptcol[m] + 1) * 128]
        lo = m + 1
        while lo <= hi:
            up = min(lo + 3, hi)
            s = product(tm, A(lo - m, up - m), 128 * (up - lo + 1), [okT[m]] + [okA[i - m] for i in range(lo, up + 1)], A(lo, up))
            for i in range(lo, up + 1):
                okA[i] = s
            lo = up + 1
        have = hi
        premultiply(have)
        if 2 * m < top:
            okT[2 * m] = product(A(m), tm, 128, [okA[m], okT[m]], T.pt[:, ptcol[2 * m] * 128:(ptcol[2 * m] + 1) * 128])
        m *= 2

    total = 0
    for k, e, dst_cores, col in sends:
        wait("g", okB[(k, e)])
        total += _write(g, core, T, topo, plan, groups, [ob((k, e))], dst_cores, col)

    s2 = inc(ve.tensor_tensor(T.x2[:], T.xs[:], T.xs[:], AluOpType.add), new())

    Y0, Y1 = T.pY0[:, 0:NB], T.pY1[:, 0:NB]
    te.matmul(Y0, A(1), x1, True, False)
    te.matmul(Y1, A(1), x0, True, False)
    sY0 = sY1 = None
    for i, (_sc, col, kind, k) in enumerate(eat):
        last = i == len(eat) - 1
        wait("te", okA[2 * k + 1])
        wait("te", okA[2 * k + 2])
        te.wait_ge(T.sem["r%d" % col], plan["inc"][(core, col)])
        blk = T.land[:, col * NB:(col + 1) * NB]
        e0, e1 = (2 * k + 1, 2 * k + 2) if kind == "F" else (2 * k + 2, 2 * k + 1)
        i0 = te.matmul(Y0, A(e0), blk, False, last)
        if last:
            sY0 = inc(i0, new())
        i1 = te.matmul(Y1, A(e1), blk, False, last)
        if last:
            sY1 = inc(i1, new())
    wait("ve", s2)
    wait("ve", sY0)
    f0 = inc(ve.tensor_tensor(T.ys[:, 0:NB], Y0, T.x2[:, 0:NB], AluOpType.add), new())
    wait("ve", sY1)
    f1 = inc(ve.tensor_tensor(T.ys[:, NB:2 * NB], Y1, T.x2[:, NB:2 * NB], AluOpType.add), new())
    wait("sy", f0)
    wait("sy", inc(sy.dma_start(T.y[:, 0:NB], T.ys[:, 0:NB]), new(16)))
    wait("sc", f1)
    wait("sc", inc(sc.dma_start(T.y[:, NB:2 * NB], T.ys[:, NB:2 * NB]), new(16)))
    g.wait_ge(T.sem.sent, total)
    for s in made:
        if not any(name == s[0] for _q, name in done):
            wait("g", s)
